import numpy as np
import ml_dtypes


def mxq(x, axis, fmt="e4m3"):
    dtype, down = {"e4m3": (ml_dtypes.float8_e4m3fn, 7), "e5m2": (ml_dtypes.float8_e5m2, 14)}[fmt]
    v = np.moveaxis(np.asarray(x, np.float32).astype(ml_dtypes.bfloat16).astype(np.float64), axis, -1)
    blocks = v.reshape(v.shape[:-1] + (-1, 32))
    amax = np.abs(blocks).max(-1, keepdims=True)
    byte = np.maximum(np.where(amax > 0, np.frexp(amax)[1] - 1 + 127, 0) - down, 1)
    scale = np.exp2(byte - 127.0)
    codes = (blocks / scale).astype(np.float32).astype(dtype).astype(np.float64)
    return np.moveaxis((codes * scale).reshape(v.shape), -1, axis)


WIDE = False


def mx_kscale(k):
    if not WIDE:
        return np.ones(k)
    levels = np.array([18, -18])
    if k % 512:
        return np.exp2(np.random.permutation(np.resize(levels, k // 32))).repeat(32)
    a = np.empty((k // 512, 16))
    for p in range(k // 512):
        a[p, :8] = np.random.permutation(np.resize(levels, 8))
        for g in range(8):
            far = levels[np.abs(levels - a[p, g]) >= 10]
            a[p, g + 8] = far[np.random.randint(len(far))]
    return np.exp2(a.ravel()).repeat(32)


def f64(x):
    return np.asarray(x).astype(np.float64)


def striped(idx):
    return np.tile(np.asarray(idx).reshape(-1, 16).T, (8, 1)).astype(np.uint16)


def unstriped(offs):
    return offs[:16].T.reshape(-1).astype(np.int64)


E2M1 = np.array([0.0, 0.5, 1.0, 1.5, 2.0, 3.0, 4.0, 6.0, -0.0, -0.5, -1.0, -1.5, -2.0, -3.0, -4.0, -6.0])


def pack_weight(w, fmt):
    k, n = w.shape
    w = f64(np.asarray(w, np.float32).astype(ml_dtypes.bfloat16)).reshape(k // 32, 32, n)
    amax = np.abs(w).max(1)
    if fmt == "e4m3":
        byte = np.frexp(amax)[1] - 1 + 127 - 7
    else:
        mant, ex = np.frexp(amax / 6.0)
        byte = np.where(mant > 0.5, ex, ex - 1) + 127
    byte = np.clip(np.where(amax > 0, byte, 1), 1, 254)
    scaled = (w * np.exp2(127.0 - byte)[:, None, :]).reshape(k, n).astype(np.float32)
    by_word = np.ascontiguousarray(scaled.reshape(k // 512, 128, 4, n).transpose(0, 1, 3, 2))
    if fmt == "e4m3":
        words = by_word.astype(ml_dtypes.float8_e4m3fn).view(np.uint8)
    else:
        c = by_word.astype(ml_dtypes.float4_e2m1fn).view(np.uint8) & 0xF
        words = (c[..., 0::2] | (c[..., 1::2] << 4)).reshape(k // 512, 128, 2 * n)
    return np.ascontiguousarray(words), np.ascontiguousarray(byte.astype(np.uint8).reshape(k // 512, 16, n))


def unpack_weight(words, scales, fmt):
    g, _, n = scales.shape
    words = np.ascontiguousarray(words).reshape(g, 128, n, -1)
    if fmt == "e4m3":
        vals = words.view(ml_dtypes.float8_e4m3fn).astype(np.float64)
    else:
        nib = np.empty((g, 128, n, 4), np.uint8)
        nib[..., 0::2] = words & 0xF
        nib[..., 1::2] = words >> 4
        vals = E2M1[nib]
    vals = vals * np.repeat(np.exp2(scales.astype(np.float64) - 127.0), 8, axis=1)[..., None]
    return vals.transpose(0, 1, 3, 2).reshape(g * 512, n)


def setup_inputs():
    n = np.random.standard_normal
    uni = np.random.uniform
    src = np.random.randint(0, 512, 1024)
    dst = np.random.randint(0, 512, 1024)
    f_d = mx_kscale(512)
    W_ = pack_weight(n((512, 512)) / np.sqrt(512) * f_d[:, None], "e2m1")
    return {
        "W_words": W_[0],
        "W_scales": W_[1],
        "hT": (n((512, 512)) / f_d[:, None]).astype(np.float32),
        "dyT": (n((512, 512)) / np.sqrt(512)).astype(np.float32),
        "soffs": striped(src),
        "toffs": striped(dst),
    }


def reference(W_words, W_scales, hT, dyT, soffs, toffs):
    src = unstriped(soffs)
    dst = unstriped(toffs)
    W = unpack_weight(W_words, W_scales, "e2m1")
    u = W.T @ mxq(f64(hT), 0, "e4m3")
    us = u[:, src]
    ds = f64(dyT)[:, dst]
    q = us * ds
    qt = q.T
    s = (qt).sum(-1, keepdims=True)
    out = s.T
    return out

@@ -1,0 +1,150 @@
+from contextlib import ExitStack
+
+import concourse.mybir as mybir
+from concourse.masks import make_identity
+
+F32 = mybir.dt.float32
+BF16 = mybir.dt.bfloat16
+I32 = mybir.dt.int32
+U32 = mybir.dt.uint32
+U16 = mybir.dt.uint16
+U8 = mybir.dt.uint8
+FP8X4 = mybir.dt.float8_e4m3fn_x4
+FP4X4 = mybir.dt.float4_e2m1fn_x4
+
+P = 128
+PACK = 4
+D, M, X, C = 512, 512, 512, 1024
+M_TILES = M // P
+HALF = X // 2
+STRIPE = 16
+BLOCK = 32
+DY_WINDOW = 1376
+U_WINDOW = 544
+PHASES = ((0, 512), (512, 896), (896, 1024))
+
+FLOPS = 2 * D * M * X
+
+
+def tile_attend_gedgew_kernel(tc, W_words, W_scales, hT, dyT, soffs, toffs, out):
+    nc = tc.nc
+    mult = mybir.AluOpType.mult
+    add = mybir.AluOpType.add
+
+    with ExitStack() as ctx:
+        lists = ctx.enter_context(tc.tile_pool(name="lists", bufs=1))
+        keep = ctx.enter_context(tc.tile_pool(name="keep", bufs=1))
+        psum = ctx.enter_context(tc.psum_pool(name="psum", bufs=1))
+
+        dst_list = lists.tile([P, C // STRIPE], U16, name="dst_list")
+        src_list = lists.tile([P, C // STRIPE], U16, name="src_list")
+
+        dy_all = keep.tile([P, (M_TILES - 1) * X + DY_WINDOW], F32, name="dy_all")
+        dy_col = [(M_TILES - 1 - j) * X for j in range(M_TILES)]
+        w_scales = keep.tile([P, M], U8, name="w_scales", align_bytes=64)
+        w_words = keep.tile([P, 2 * M], U8, name="w_words", align_bytes=64)
+        h_raw = [keep.tile([P, PACK, HALF], F32, name="h_raw%d" % a, tag="h_raw%d" % a) for a in range(2)]
+        h_bf = keep.tile([P, X, PACK], BF16, name="h_bf", align_bytes=64)
+        h_codes = keep.tile([P, X], U32, name="h_codes", align_bytes=64)
+        h_scales = keep.tile([P, X], U8, name="h_scales", align_bytes=64)
+        u = [keep.tile([P, U_WINDOW], F32, name="u%d" % j) for j in range(M_TILES)]
+        ident = keep.tile([P, P], F32, name="ident")
+        sums = keep.tile([P, (C // P) * BLOCK], F32, name="sums", align_bytes=64)
+        sums_t = keep.tile([P, (C // P) * BLOCK], F32, name="sums_t", align_bytes=64)
+        scratch = keep.tile([P, P], F32, name="scratch")
+
+        nc.vector.memset(w_scales[:].bitcast(I32), 0)
+        nc.vector.memset(dy_all[:, M_TILES * X :], 0.0)
+        make_identity(nc, ident[:])
+        nc.gpsimd.memset(sums[:], 0.0)
+        for j in range(M_TILES):
+            nc.gpsimd.memset(u[j][:, X:], 0.0)
+
+        def load_dy(j):
+            nc.sync.dma_start(out=dy_all[:, dy_col[j] : dy_col[j] + X], in_=dyT[j * P : (j + 1) * P, :])
+
+        h_rows = hT.rearrange("(p t) x -> p t x", t=PACK)
+        load_dy(0)
+        nc.sync.dma_start(dst_list[:], toffs)
+        load_dy(1)
+        for a in range(2):
+            nc.sync.dma_start(out=h_raw[a][:], in_=h_rows[:, :, a * HALF : (a + 1) * HALF])
+        load_dy(2)
+        nc.sync.dma_start(out=w_words[:].bitcast(I32), in_=W_words[0].bitcast(I32))
+        for quad in range(4):
+            nc.sync.dma_start(
+                out=w_scales[32 * quad : 32 * quad + 4, :].bitcast(I32),
+                in_=W_scales[0, 4 * quad : 4 * quad + 4, :].bitcast(I32),
+            )
+        load_dy(3)
+        nc.sync.dma_start(src_list[:], soffs)
+
+        for a in range(2):
+            nc.scalar.copy(
+                out=h_bf[:, a * HALF : (a + 1) * HALF, :].rearrange("p (c i) t -> p c t i", i=4),
+                in_=h_raw[a][:].rearrange("p t (c i) -> p c t i", i=4),
+            )
+
+        dy_edge = []
+
+        def gather_dy(j, tag):
+            g = keep.tile([P, C], F32, name="dy_edge%d" % j, tag=tag)
+            nc.vector.tensor_copy(g[:], dy_all[:, dy_col[j] : dy_col[j] + DY_WINDOW].indirect(dst_list[:]))
+            dy_edge.append(g)
+
+        for j in range(M_TILES - 1):
+            gather_dy(j, "dy_edge%d" % j)
+        nc.vector.quantize_mx(
+            out=h_codes[:].bitcast(FP8X4), scales=h_scales[:], in_=h_bf[:].rearrange("p x t -> p (x t)")
+        )
+        gather_dy(M_TILES - 1, "h_raw1")
+
+        for j in range(M_TILES):
+            u_bank = psum.tile([P, X], F32, name="u_bank%d" % j)
+            nc.tensor.matmul_mx(
+                out=u_bank[:],
+                lhsT=w_words[:, 2 * P * j : 2 * P * (j + 1)].bitcast(FP4X4),
+                lhsT_scale=w_scales[:, P * j : P * (j + 1)],
+                rhs=h_codes[:].bitcast(FP8X4),
+                rhs_scale=h_scales[:],
+                start=True,
+                stop=True,
+            )
+            nc.scalar.copy(out=u[j][:, :X], in_=u_bank[:])
+
+        for ph, (c0, c1) in enumerate(PHASES):
+            chunks = (c1 - c0) // P
+            acc = psum.tile([P, c1 - c0], F32, name="acc%d" % ph)
+            for j in range(M_TILES):
+                q = keep.tile([P, c1 - c0], F32, name="q%d_%d" % (ph, j))
+                nc.vector.tensor_tensor(
+                    q[:], u[j][:].indirect(src_list[:, c0 // STRIPE : c1 // STRIPE]), dy_edge[j][:, c0:c1], mult
+                )
+                for i in range(chunks):
+                    nc.tensor.matmul(
+                        acc[:, i * P : (i + 1) * P],
+                        q[:, i * P : (i + 1) * P],
+                        ident[:],
+                        start=(j == 0 and i == 0),
+                        stop=(j == M_TILES - 1 and i == chunks - 1),
+                        is_transpose=True,
+                    )
+            for i in range(chunks):
+                col = (c0 // P + i) * BLOCK
+                if ph < len(PHASES) - 1:
+                    nc.scalar.activation(
+                        out=scratch[:],
+                        in_=acc[:, i * P : (i + 1) * P],
+                        func=mybir.ActivationFunctionType.Copy,
+                        accum_out=sums[:, col : col + 1],
+                    )
+                else:
+                    nc.vector.tensor_reduce(
+                        out=sums[:, col : col + 1], in_=acc[:, i * P : (i + 1) * P], axis=mybir.AxisListType.X, op=add
+                    )
+
+        nc.vector.transpose(sums_t[:], sums[:])
+        nc.sync.dma_start(
+            out=out.rearrange("o (j b q) -> b (o j) q", b=P // BLOCK, q=BLOCK),
+            in_=sums_t[0:P:BLOCK, :].rearrange("b (j q) -> b j q", q=BLOCK),
+        )

@@ -20,7 +20,7 @@ HALF = X // 2
 STRIPE = 16
 BLOCK = 32
 DY_WINDOW = 1376
-U_WINDOW = 544
+U_WINDOWS = (1040, 912, 528, 528)
 PHASES = ((0, 512), (512, 896), (896, 1024))
 
 FLOPS = 2 * D * M * X
@@ -47,16 +47,18 @@ def tile_attend_gedgew_kernel(tc, W_words, W_scales, hT, dyT, soffs, toffs, out)
         h_bf = keep.tile([P, X, PACK], BF16, name="h_bf", align_bytes=64)
         h_codes = keep.tile([P, X], U32, name="h_codes", align_bytes=64)
         h_scales = keep.tile([P, X], U8, name="h_scales", align_bytes=64)
-        u = [keep.tile([P, U_WINDOW], F32, name="u%d" % j) for j in range(M_TILES)]
+        u = [keep.tile([P, U_WINDOWS[j]], F32, name="u%d" % j) for j in range(M_TILES)]
         ident = keep.tile([P, P], F32, name="ident")
-        sums = keep.tile([P, (C // P) * BLOCK], F32, name="sums", align_bytes=64)
-        sums_t = keep.tile([P, (C // P) * BLOCK], F32, name="sums_t", align_bytes=64)
-        scratch = keep.tile([P, P], F32, name="scratch")
+        sums = keep.tile([P, 4 * BLOCK], F32, name="sums", align_bytes=64)
+        sums_t = keep.tile([P, 4 * BLOCK], F32, name="sums_t", align_bytes=64)
+        early = keep.tile([P, P], F32, name="early")
+        scratch = keep.tile([P, C], F32, name="scratch")
 
         nc.vector.memset(w_scales[:].bitcast(I32), 0)
         nc.vector.memset(dy_all[:, M_TILES * X :], 0.0)
         make_identity(nc, ident[:])
         nc.gpsimd.memset(sums[:], 0.0)
+        nc.gpsimd.memset(early[:], 0.0)
         for j in range(M_TILES):
             nc.gpsimd.memset(u[j][:, X:], 0.0)
 
@@ -112,39 +114,57 @@ def tile_attend_gedgew_kernel(tc, W_words, W_scales, hT, dyT, soffs, toffs, out)
             )
             nc.scalar.copy(out=u[j][:, :X], in_=u_bank[:])
 
-        for ph, (c0, c1) in enumerate(PHASES):
-            chunks = (c1 - c0) // P
-            acc = psum.tile([P, c1 - c0], F32, name="acc%d" % ph)
-            for j in range(M_TILES):
-                q = keep.tile([P, c1 - c0], F32, name="q%d_%d" % (ph, j))
-                nc.vector.tensor_tensor(
-                    q[:], u[j][:].indirect(src_list[:, c0 // STRIPE : c1 // STRIPE]), dy_edge[j][:, c0:c1], mult
-                )
-                for i in range(chunks):
-                    nc.tensor.matmul(
-                        acc[:, i * P : (i + 1) * P],
-                        q[:, i * P : (i + 1) * P],
-                        ident[:],
-                        start=(j == 0 and i == 0),
-                        stop=(j == M_TILES - 1 and i == chunks - 1),
-                        is_transpose=True,
-                    )
-            for i in range(chunks):
-                col = (c0 // P + i) * BLOCK
-                if ph < len(PHASES) - 1:
-                    nc.scalar.activation(
-                        out=scratch[:],
-                        in_=acc[:, i * P : (i + 1) * P],
-                        func=mybir.ActivationFunctionType.Copy,
-                        accum_out=sums[:, col : col + 1],
-                    )
-                else:
-                    nc.vector.tensor_reduce(
-                        out=sums[:, col : col + 1], in_=acc[:, i * P : (i + 1) * P], axis=mybir.AxisListType.X, op=add
-                    )
+        accs = [psum.tile([P, c1 - c0], F32, name="acc%d" % ph) for ph, (c0, c1) in enumerate(PHASES)]
+        phase_of = [ph for ph, (c0, c1) in enumerate(PHASES) for c in range(c0, c1, P)]
 
+        def products(j, c0, c1):
+            q = keep.tile([P, c1 - c0], F32, name="q%d_%d" % (j, c0))
+            nc.vector.tensor_tensor(
+                q[:], u[j][:].indirect(src_list[:, c0 // STRIPE : c1 // STRIPE]), dy_edge[j][:, c0:c1], mult
+            )
+            for c in range(c0, c1, P):
+                ph = phase_of[c // P]
+                lo, hi = PHASES[ph]
+                nc.tensor.matmul(
+                    accs[ph][:, c - lo : c - lo + P],
+                    q[:, c - c0 : c - c0 + P],
+                    ident[:],
+                    start=(j == 0 and c == lo),
+                    stop=(j == M_TILES - 1 and c + P == hi),
+                    is_transpose=True,
+                )
+
+        def scalar_sum(ph, i, dst):
+            nc.scalar.activation(
+                out=scratch[:, PHASES[ph][0] + i * P : PHASES[ph][0] + (i + 1) * P],
+                in_=accs[ph][:, i * P : (i + 1) * P],
+                func=mybir.ActivationFunctionType.Copy,
+                accum_out=dst,
+            )
+
+        (a0, a1), (b0, b1), (c0, c1) = PHASES
+        products(0, a0, c1)
+        products(1, a0, b1)
+        products(2, a0, a1)
+        products(3, a0, a1)
+        for i in range(4):
+            scalar_sum(0, i, early[:, i : i + 1])
+        products(2, b0, b1)
+        early_t = psum.tile([P, P], F32, name="early_t")
+        nc.tensor.transpose(early_t[:], early[:], ident[:])
+        early_rows = keep.tile([BLOCK, P], F32, name="early_rows")
+        nc.scalar.copy(out=early_rows[:], in_=early_t[0:BLOCK, :])
+        nc.sync.dma_start(out=out[:, a0:a1].rearrange("o (i p) -> (o i) p", p=P), in_=early_rows[0:4, :])
+        products(3, b0, b1)
+        for i in range(3):
+            scalar_sum(1, i, sums[:, i * BLOCK : i * BLOCK + 1])
+        for j in range(1, M_TILES):
+            products(j, c0, c1)
+        nc.vector.tensor_reduce(
+            out=sums[:, 3 * BLOCK : 3 * BLOCK + 1], in_=accs[2][:], axis=mybir.AxisListType.X, op=add
+        )
         nc.vector.transpose(sums_t[:], sums[:])
         nc.sync.dma_start(
-            out=out.rearrange("o (j b q) -> b (o j) q", b=P // BLOCK, q=BLOCK),
+            out=out[:, b0:c1].rearrange("o (j b q) -> b (o j) q", b=P // BLOCK, q=BLOCK),
             in_=sums_t[0:P:BLOCK, :].rearrange("b (j q) -> b j q", q=BLOCK),
         )

@@ -19,9 +19,14 @@ M_TILES = M // P
 HALF = X // 2
 STRIPE = 16
 BLOCK = 32
+BANK = 512
 DY_WINDOW = 1376
-U_WINDOWS = (1040, 912, 528, 528)
-PHASES = ((0, 512), (512, 896), (896, 1024))
+EARLY = 640
+EARLY_T = 256
+LATE_T = 128
+LATE_COL = EARLY_T - 16
+U_WINDOWS = (1040, 1040, 656, 656)
+GROUPS = ((0, 384), (384, 640), (640, 768), (768, 1024))
 
 FLOPS = 2 * D * M * X
 
@@ -49,36 +54,35 @@ def tile_attend_gedgew_kernel(tc, W_words, W_scales, hT, dyT, soffs, toffs, out)
         h_scales = keep.tile([P, X], U8, name="h_scales", align_bytes=64)
         u = [keep.tile([P, U_WINDOWS[j]], F32, name="u%d" % j) for j in range(M_TILES)]
         ident = keep.tile([P, P], F32, name="ident")
-        sums = keep.tile([P, 4 * BLOCK], F32, name="sums", align_bytes=64)
-        sums_t = keep.tile([P, 4 * BLOCK], F32, name="sums_t", align_bytes=64)
-        early = keep.tile([P, P], F32, name="early")
+        sums = keep.tile([P, LATE_COL + LATE_T], F32, name="sums", align_bytes=64)
+        early_rows = keep.tile([P, EARLY_T], F32, name="early_rows", align_bytes=64)
+        late_rows = keep.tile([P, LATE_T], F32, name="late_rows", align_bytes=64)
         scratch = keep.tile([P, C], F32, name="scratch")
 
         nc.vector.memset(w_scales[:].bitcast(I32), 0)
         nc.vector.memset(dy_all[:, M_TILES * X :], 0.0)
         make_identity(nc, ident[:])
         nc.gpsimd.memset(sums[:], 0.0)
-        nc.gpsimd.memset(early[:], 0.0)
         for j in range(M_TILES):
             nc.gpsimd.memset(u[j][:, X:], 0.0)
 
-        def load_dy(j):
-            nc.sync.dma_start(out=dy_all[:, dy_col[j] : dy_col[j] + X], in_=dyT[j * P : (j + 1) * P, :])
+        def load_dy(j, queue):
+            queue.dma_start(out=dy_all[:, dy_col[j] : dy_col[j] + X], in_=dyT[j * P : (j + 1) * P, :])
 
         h_rows = hT.rearrange("(p t) x -> p t x", t=PACK)
-        load_dy(0)
+        load_dy(0, nc.sync)
         nc.sync.dma_start(dst_list[:], toffs)
-        load_dy(1)
+        load_dy(1, nc.sync)
         for a in range(2):
             nc.sync.dma_start(out=h_raw[a][:], in_=h_rows[:, :, a * HALF : (a + 1) * HALF])
-        load_dy(2)
+        load_dy(2, nc.sync)
         nc.sync.dma_start(out=w_words[:].bitcast(I32), in_=W_words[0].bitcast(I32))
         for quad in range(4):
             nc.sync.dma_start(
                 out=w_scales[32 * quad : 32 * quad + 4, :].bitcast(I32),
                 in_=W_scales[0, 4 * quad : 4 * quad + 4, :].bitcast(I32),
             )
-        load_dy(3)
+        load_dy(3, nc.sync)
         nc.sync.dma_start(src_list[:], soffs)
 
         for a in range(2):
@@ -114,8 +118,8 @@ def tile_attend_gedgew_kernel(tc, W_words, W_scales, hT, dyT, soffs, toffs, out)
             )
             nc.scalar.copy(out=u[j][:, :X], in_=u_bank[:])
 
-        accs = [psum.tile([P, c1 - c0], F32, name="acc%d" % ph) for ph, (c0, c1) in enumerate(PHASES)]
-        phase_of = [ph for ph, (c0, c1) in enumerate(PHASES) for c in range(c0, c1, P)]
+        accs = [psum.tile([P, c1 - c0], F32, name="acc%d" % g) for g, (c0, c1) in enumerate(GROUPS)]
+        group_of = {c: g for g, (c0, c1) in enumerate(GROUPS) for c in range(c0, c1, P)}
 
         def products(j, c0, c1):
             q = keep.tile([P, c1 - c0], F32, name="q%d_%d" % (j, c0))
@@ -123,10 +127,10 @@ def tile_attend_gedgew_kernel(tc, W_words, W_scales, hT, dyT, soffs, toffs, out)
                 q[:], u[j][:].indirect(src_list[:, c0 // STRIPE : c1 // STRIPE]), dy_edge[j][:, c0:c1], mult
             )
             for c in range(c0, c1, P):
-                ph = phase_of[c // P]
-                lo, hi = PHASES[ph]
+                g = group_of[c]
+                lo, hi = GROUPS[g]
                 nc.tensor.matmul(
-                    accs[ph][:, c - lo : c - lo + P],
+                    accs[g][:, c - lo : c - lo + P],
                     q[:, c - c0 : c - c0 + P],
                     ident[:],
                     start=(j == 0 and c == lo),
@@ -134,37 +138,40 @@ def tile_attend_gedgew_kernel(tc, W_words, W_scales, hT, dyT, soffs, toffs, out)
                     is_transpose=True,
                 )
 
-        def scalar_sum(ph, i, dst):
-            nc.scalar.activation(
-                out=scratch[:, PHASES[ph][0] + i * P : PHASES[ph][0] + (i + 1) * P],
-                in_=accs[ph][:, i * P : (i + 1) * P],
-                func=mybir.ActivationFunctionType.Copy,
-                accum_out=dst,
+        def sum_column(c):
+            return c // P * BLOCK if c < EARLY else LATE_COL + (c - EARLY) // P * BLOCK
+
+        def scalar_sums(c0, c1):
+            for c in range(c0, c1, P):
+                g = group_of[c]
+                lo = GROUPS[g][0]
+                nc.scalar.activation(
+                    out=scratch[:, c : c + P],
+                    in_=accs[g][:, c - lo : c - lo + P],
+                    func=mybir.ActivationFunctionType.Copy,
+                    accum_out=sums[:, sum_column(c) : sum_column(c) + 1],
+                )
+
+        def store(rows, c0, c1):
+            nc.sync.dma_start(
+                out=out[:, c0:c1].rearrange("o (j b q) -> b (o j) q", b=P // BLOCK, q=BLOCK),
+                in_=rows[0:P:BLOCK, : (c1 - c0) // P * BLOCK].rearrange("b (j q) -> b j q", q=BLOCK),
             )
 
-        (a0, a1), (b0, b1), (c0, c1) = PHASES
-        products(0, a0, c1)
-        products(1, a0, b1)
-        products(2, a0, a1)
-        products(3, a0, a1)
-        for i in range(4):
-            scalar_sum(0, i, early[:, i : i + 1])
-        products(2, b0, b1)
-        early_t = psum.tile([P, P], F32, name="early_t")
-        nc.tensor.transpose(early_t[:], early[:], ident[:])
-        early_rows = keep.tile([BLOCK, P], F32, name="early_rows")
-        nc.scalar.copy(out=early_rows[:], in_=early_t[0:BLOCK, :])
-        nc.sync.dma_start(out=out[:, a0:a1].rearrange("o (i p) -> (o i) p", p=P), in_=early_rows[0:4, :])
-        products(3, b0, b1)
-        for i in range(3):
-            scalar_sum(1, i, sums[:, i * BLOCK : i * BLOCK + 1])
-        for j in range(1, M_TILES):
-            products(j, c0, c1)
+        last = EARLY + P
+        products(0, 0, C)
+        products(1, 0, C)
+        products(2, 0, EARLY)
+        products(3, 0, EARLY)
+        scalar_sums(0, EARLY)
+        products(2, EARLY, C)
+        products(3, last, C)
+        scalar_sums(last, C)
+        products(3, EARLY, last)
+        nc.vector.transpose(early_rows[:], sums[:, :EARLY_T])
+        store(early_rows, 0, EARLY)
         nc.vector.tensor_reduce(
-            out=sums[:, 3 * BLOCK : 3 * BLOCK + 1], in_=accs[2][:], axis=mybir.AxisListType.X, op=add
+            out=sums[:, LATE_COL : LATE_COL + 1], in_=accs[group_of[EARLY]][:], axis=mybir.AxisListType.X, op=add
         )
-        nc.vector.transpose(sums_t[:], sums[:])
-        nc.sync.dma_start(
-            out=out[:, b0:c1].rearrange("o (j b q) -> b (o j) q", b=P // BLOCK, q=BLOCK),
-            in_=sums_t[0:P:BLOCK, :].rearrange("b (j q) -> b j q", q=BLOCK),
-        )
+        nc.vector.transpose(late_rows[:], sums[:, LATE_COL : LATE_COL + LATE_T])
+        store(late_rows, EARLY, C)

@@ -59,12 +59,14 @@ def tile_attend_gedgew_kernel(tc, W_words, W_scales, hT, dyT, soffs, toffs, out)
         late_rows = keep.tile([P, LATE_T], F32, name="late_rows", align_bytes=64)
         scratch = keep.tile([P, C], F32, name="scratch")
 
-        nc.vector.memset(w_scales[:].bitcast(I32), 0)
+        zero = keep.tile([P, 1], F32, name="zero")
+        nc.vector.memset(zero[:], 0.0)
         nc.vector.memset(dy_all[:, M_TILES * X :], 0.0)
+        nc.vector.memset(w_scales[:].bitcast(I32), 0)
         make_identity(nc, ident[:])
-        nc.gpsimd.memset(sums[:], 0.0)
         for j in range(M_TILES):
-            nc.gpsimd.memset(u[j][:, X:], 0.0)
+            nc.scalar.copy(out=u[j][:, X:], in_=zero[:].to_broadcast([P, U_WINDOWS[j] - X]))
+        nc.scalar.copy(out=sums[:], in_=zero[:].to_broadcast([P, LATE_COL + LATE_T]))
 
         def load_dy(j, queue):
             queue.dma_start(out=dy_all[:, dy_col[j] : dy_col[j] + X], in_=dyT[j * P : (j + 1) * P, :])

@@ -21,12 +21,9 @@ STRIPE = 16
 BLOCK = 32
 BANK = 512
 DY_WINDOW = 1376
-EARLY = 640
-EARLY_T = 256
-LATE_T = 128
-LATE_COL = EARLY_T - 16
-U_WINDOWS = (1040, 1040, 656, 656)
-GROUPS = ((0, 384), (384, 640), (640, 768), (768, 1024))
+U_WINDOWS = (1040, 1040, 528, 528)
+GROUPS = ((0, 256), (256, 512), (512, 896), (896, 1024))
+EARLY, LAST = 512, 896
 
 FLOPS = 2 * D * M * X
 
@@ -54,9 +51,8 @@ def tile_attend_gedgew_kernel(tc, W_words, W_scales, hT, dyT, soffs, toffs, out)
         h_scales = keep.tile([P, X], U8, name="h_scales", align_bytes=64)
         u = [keep.tile([P, U_WINDOWS[j]], F32, name="u%d" % j) for j in range(M_TILES)]
         ident = keep.tile([P, P], F32, name="ident")
-        sums = keep.tile([P, LATE_COL + LATE_T], F32, name="sums", align_bytes=64)
-        early_rows = keep.tile([P, EARLY_T], F32, name="early_rows", align_bytes=64)
-        late_rows = keep.tile([P, LATE_T], F32, name="late_rows", align_bytes=64)
+        sums = keep.tile([P, (C // P + 1) * BLOCK], F32, name="sums", align_bytes=64)
+        rows = keep.tile([P, (C // P + 1) * BLOCK], F32, name="rows", align_bytes=64)
         scratch = keep.tile([P, C], F32, name="scratch")
 
         zero = keep.tile([P, 1], F32, name="zero")
@@ -66,7 +62,7 @@ def tile_attend_gedgew_kernel(tc, W_words, W_scales, hT, dyT, soffs, toffs, out)
         make_identity(nc, ident[:])
         for j in range(M_TILES):
             nc.scalar.copy(out=u[j][:, X:], in_=zero[:].to_broadcast([P, U_WINDOWS[j] - X]))
-        nc.scalar.copy(out=sums[:], in_=zero[:].to_broadcast([P, LATE_COL + LATE_T]))
+        nc.scalar.copy(out=sums[:], in_=zero[:].to_broadcast([P, (C // P + 1) * BLOCK]))
 
         def load_dy(j, queue):
             queue.dma_start(out=dy_all[:, dy_col[j] : dy_col[j] + X], in_=dyT[j * P : (j + 1) * P, :])
@@ -140,9 +136,6 @@ def tile_attend_gedgew_kernel(tc, W_words, W_scales, hT, dyT, soffs, toffs, out)
                     is_transpose=True,
                 )
 
-        def sum_column(c):
-            return c // P * BLOCK if c < EARLY else LATE_COL + (c - EARLY) // P * BLOCK
-
         def scalar_sums(c0, c1):
             for c in range(c0, c1, P):
                 g = group_of[c]
@@ -151,29 +144,42 @@ def tile_attend_gedgew_kernel(tc, W_words, W_scales, hT, dyT, soffs, toffs, out)
                     out=scratch[:, c : c + P],
                     in_=accs[g][:, c - lo : c - lo + P],
                     func=mybir.ActivationFunctionType.Copy,
-                    accum_out=sums[:, sum_column(c) : sum_column(c) + 1],
+                    accum_out=sums[:, c // P * BLOCK : c // P * BLOCK + 1],
                 )
 
-        def store(rows, c0, c1):
-            nc.sync.dma_start(
-                out=out[:, c0:c1].rearrange("o (j b q) -> b (o j) q", b=P // BLOCK, q=BLOCK),
-                in_=rows[0:P:BLOCK, : (c1 - c0) // P * BLOCK].rearrange("b (j q) -> b j q", q=BLOCK),
+        def vector_sums(g, block):
+            lo, hi = GROUPS[g]
+            nc.vector.tensor_reduce(
+                out=sums[:, block * BLOCK : (block + (hi - lo) // P) * BLOCK : BLOCK],
+                in_=accs[g][:].rearrange("p (k m) -> p k m", m=P),
+                axis=mybir.AxisListType.X,
+                op=add,
             )
 
-        last = EARLY + P
+        def turn(b0, b1):
+            cols = slice(b0 * BLOCK, b1 * BLOCK)
+            nc.vector.transpose(rows[:, cols], sums[:, cols])
+
+        def store(queue, block, c0, c1):
+            queue.dma_start(
+                out=out[:, c0:c1].rearrange("o (j b q) -> b (o j) q", b=P // BLOCK, q=BLOCK),
+                in_=rows[0:P:BLOCK, block * BLOCK : (block + (c1 - c0) // P) * BLOCK].rearrange("b (j q) -> b j q", q=BLOCK),
+            )
+
         products(0, 0, C)
         products(1, 0, C)
         products(2, 0, EARLY)
         products(3, 0, EARLY)
         scalar_sums(0, EARLY)
-        products(2, EARLY, C)
-        products(3, last, C)
-        scalar_sums(last, C)
-        products(3, EARLY, last)
-        nc.vector.transpose(early_rows[:], sums[:, :EARLY_T])
-        store(early_rows, 0, EARLY)
-        nc.vector.tensor_reduce(
-            out=sums[:, LATE_COL : LATE_COL + 1], in_=accs[group_of[EARLY]][:], axis=mybir.AxisListType.X, op=add
-        )
-        nc.vector.transpose(late_rows[:], sums[:, LATE_COL : LATE_COL + LATE_T])
-        store(late_rows, EARLY, C)
+        products(2, EARLY, LAST)
+        products(3, EARLY, LAST)
+        products(2, LAST, C)
+        products(3, LAST, C)
+        turn(0, 4)
+        store(nc.sync, 0, 0, EARLY)
+        vector_sums(2, 4)
+        vector_sums(3, 8)
+        turn(4, 8)
+        store(nc.scalar, 4, EARLY, LAST)
+        turn(8, 9)
+        store(nc.sync, 8, LAST, C)

@@ -19,11 +19,12 @@ M_TILES = M // P
 HALF = X // 2
 STRIPE = 16
 BLOCK = 32
-BANK = 512
 DY_WINDOW = 1376
-U_WINDOWS = (1040, 1040, 528, 528)
+SHORT_WINDOW = 704
+LAST = C - P
+EARLY = 512
+U_WINDOWS = (1040, 1040, 912, 528)
 GROUPS = ((0, 256), (256, 512), (512, 896), (896, 1024))
-EARLY, LAST = 512, 896
 
 FLOPS = 2 * D * M * X
 
@@ -43,6 +44,7 @@ def tile_attend_gedgew_kernel(tc, W_words, W_scales, hT, dyT, soffs, toffs, out)
 
         dy_all = keep.tile([P, (M_TILES - 1) * X + DY_WINDOW], F32, name="dy_all")
         dy_col = [(M_TILES - 1 - j) * X for j in range(M_TILES)]
+        dy_edge = [keep.tile([P, C], F32, name="dy_edge%d" % j) for j in range(M_TILES - 1)]
         w_scales = keep.tile([P, M], U8, name="w_scales", align_bytes=64)
         w_words = keep.tile([P, 2 * M], U8, name="w_words", align_bytes=64)
         h_raw = [keep.tile([P, PACK, HALF], F32, name="h_raw%d" % a, tag="h_raw%d" % a) for a in range(2)]
@@ -51,36 +53,36 @@ def tile_attend_gedgew_kernel(tc, W_words, W_scales, hT, dyT, soffs, toffs, out)
         h_scales = keep.tile([P, X], U8, name="h_scales", align_bytes=64)
         u = [keep.tile([P, U_WINDOWS[j]], F32, name="u%d" % j) for j in range(M_TILES)]
         ident = keep.tile([P, P], F32, name="ident")
-        sums = keep.tile([P, (C // P + 1) * BLOCK], F32, name="sums", align_bytes=64)
-        rows = keep.tile([P, (C // P + 1) * BLOCK], F32, name="rows", align_bytes=64)
+        zero = keep.tile([P, 1], F32, name="zero")
+        sums = keep.tile([P, 9 * BLOCK], F32, name="sums", align_bytes=64)
+        rows = keep.tile([P, 9 * BLOCK], F32, name="rows", align_bytes=64)
         scratch = keep.tile([P, C], F32, name="scratch")
 
-        zero = keep.tile([P, 1], F32, name="zero")
         nc.vector.memset(zero[:], 0.0)
         nc.vector.memset(dy_all[:, M_TILES * X :], 0.0)
         nc.vector.memset(w_scales[:].bitcast(I32), 0)
         make_identity(nc, ident[:])
         for j in range(M_TILES):
             nc.scalar.copy(out=u[j][:, X:], in_=zero[:].to_broadcast([P, U_WINDOWS[j] - X]))
-        nc.scalar.copy(out=sums[:], in_=zero[:].to_broadcast([P, (C // P + 1) * BLOCK]))
+        nc.scalar.copy(out=sums[:], in_=zero[:].to_broadcast([P, 9 * BLOCK]))
 
-        def load_dy(j, queue):
-            queue.dma_start(out=dy_all[:, dy_col[j] : dy_col[j] + X], in_=dyT[j * P : (j + 1) * P, :])
+        def load_dy(j):
+            nc.sync.dma_start(out=dy_all[:, dy_col[j] : dy_col[j] + X], in_=dyT[j * P : (j + 1) * P, :])
 
         h_rows = hT.rearrange("(p t) x -> p t x", t=PACK)
-        load_dy(0, nc.sync)
+        load_dy(0)
         nc.sync.dma_start(dst_list[:], toffs)
-        load_dy(1, nc.sync)
+        load_dy(1)
         for a in range(2):
             nc.sync.dma_start(out=h_raw[a][:], in_=h_rows[:, :, a * HALF : (a + 1) * HALF])
-        load_dy(2, nc.sync)
+        load_dy(2)
         nc.sync.dma_start(out=w_words[:].bitcast(I32), in_=W_words[0].bitcast(I32))
         for quad in range(4):
             nc.sync.dma_start(
                 out=w_scales[32 * quad : 32 * quad + 4, :].bitcast(I32),
                 in_=W_scales[0, 4 * quad : 4 * quad + 4, :].bitcast(I32),
             )
-        load_dy(3, nc.sync)
+        load_dy(3)
         nc.sync.dma_start(src_list[:], soffs)
 
         for a in range(2):
@@ -89,22 +91,21 @@ def tile_attend_gedgew_kernel(tc, W_words, W_scales, hT, dyT, soffs, toffs, out)
                 in_=h_raw[a][:].rearrange("p t (c i) -> p c t i", i=4),
             )
 
-        dy_edge = []
-
-        def gather_dy(j, tag):
-            g = keep.tile([P, C], F32, name="dy_edge%d" % j, tag=tag)
-            nc.vector.tensor_copy(g[:], dy_all[:, dy_col[j] : dy_col[j] + DY_WINDOW].indirect(dst_list[:]))
-            dy_edge.append(g)
+        def gather_dy(j, dst, c0, c1, window):
+            nc.vector.tensor_copy(
+                dst, dy_all[:, dy_col[j] : dy_col[j] + window].indirect(dst_list[:, c0 // STRIPE : c1 // STRIPE])
+            )
 
         for j in range(M_TILES - 1):
-            gather_dy(j, "dy_edge%d" % j)
+            gather_dy(j, dy_edge[j][:], 0, C, DY_WINDOW)
         nc.vector.quantize_mx(
             out=h_codes[:].bitcast(FP8X4), scales=h_scales[:], in_=h_bf[:].rearrange("p x t -> p (x t)")
         )
-        gather_dy(M_TILES - 1, "h_raw1")
+        dy_last = keep.tile([P, C], F32, name="dy_last", tag="h_raw1")
+        gather_dy(M_TILES - 1, dy_last[:, :LAST], 0, LAST, DY_WINDOW)
 
         for j in range(M_TILES):
-            u_bank = psum.tile([P, X], F32, name="u_bank%d" % j)
+            u_bank = psum.tile([P, X], F32, name="u_bank%d" % j, tag="bank%d" % j)
             nc.tensor.matmul_mx(
                 out=u_bank[:],
                 lhsT=w_words[:, 2 * P * j : 2 * P * (j + 1)].bitcast(FP4X4),
@@ -116,14 +117,15 @@ def tile_attend_gedgew_kernel(tc, W_words, W_scales, hT, dyT, soffs, toffs, out)
             )
             nc.scalar.copy(out=u[j][:, :X], in_=u_bank[:])
 
-        accs = [psum.tile([P, c1 - c0], F32, name="acc%d" % g) for g, (c0, c1) in enumerate(GROUPS)]
+        accs = [
+            psum.tile([P, c1 - c0], F32, name="acc%d" % g, tag="bank%d" % ((M_TILES + g) % 8))
+            for g, (c0, c1) in enumerate(GROUPS)
+        ]
         group_of = {c: g for g, (c0, c1) in enumerate(GROUPS) for c in range(c0, c1, P)}
 
-        def products(j, c0, c1):
+        def products(j, c0, c1, dy):
             q = keep.tile([P, c1 - c0], F32, name="q%d_%d" % (j, c0))
-            nc.vector.tensor_tensor(
-                q[:], u[j][:].indirect(src_list[:, c0 // STRIPE : c1 // STRIPE]), dy_edge[j][:, c0:c1], mult
-            )
+            nc.vector.tensor_tensor(q[:], u[j][:].indirect(src_list[:, c0 // STRIPE : c1 // STRIPE]), dy, mult)
             for c in range(c0, c1, P):
                 g = group_of[c]
                 lo, hi = GROUPS[g]
@@ -136,21 +138,23 @@ def tile_attend_gedgew_kernel(tc, W_words, W_scales, hT, dyT, soffs, toffs, out)
                     is_transpose=True,
                 )
 
-        def scalar_sums(c0, c1):
-            for c in range(c0, c1, P):
-                g = group_of[c]
-                lo = GROUPS[g][0]
+        def block_of(c):
+            return c // P if c < LAST else 8
+
+        def scalar_sums(g):
+            lo, hi = GROUPS[g]
+            for c in range(lo, hi, P):
                 nc.scalar.activation(
                     out=scratch[:, c : c + P],
                     in_=accs[g][:, c - lo : c - lo + P],
                     func=mybir.ActivationFunctionType.Copy,
-                    accum_out=sums[:, c // P * BLOCK : c // P * BLOCK + 1],
+                    accum_out=sums[:, block_of(c) * BLOCK : block_of(c) * BLOCK + 1],
                 )
 
-        def vector_sums(g, block):
+        def vector_sums(g):
             lo, hi = GROUPS[g]
             nc.vector.tensor_reduce(
-                out=sums[:, block * BLOCK : (block + (hi - lo) // P) * BLOCK : BLOCK],
+                out=sums[:, block_of(lo) * BLOCK : (block_of(lo) + (hi - lo) // P) * BLOCK : BLOCK],
                 in_=accs[g][:].rearrange("p (k m) -> p k m", m=P),
                 axis=mybir.AxisListType.X,
                 op=add,
@@ -160,26 +164,28 @@ def tile_attend_gedgew_kernel(tc, W_words, W_scales, hT, dyT, soffs, toffs, out)
             cols = slice(b0 * BLOCK, b1 * BLOCK)
             nc.vector.transpose(rows[:, cols], sums[:, cols])
 
-        def store(queue, block, c0, c1):
+        def store(queue, c0, c1):
+            b0 = block_of(c0)
             queue.dma_start(
                 out=out[:, c0:c1].rearrange("o (j b q) -> b (o j) q", b=P // BLOCK, q=BLOCK),
-                in_=rows[0:P:BLOCK, block * BLOCK : (block + (c1 - c0) // P) * BLOCK].rearrange("b (j q) -> b j q", q=BLOCK),
+                in_=rows[0:P:BLOCK, b0 * BLOCK : (b0 + (c1 - c0) // P) * BLOCK].rearrange("b (j q) -> b j q", q=BLOCK),
             )
 
-        products(0, 0, C)
-        products(1, 0, C)
-        products(2, 0, EARLY)
-        products(3, 0, EARLY)
-        scalar_sums(0, EARLY)
-        products(2, EARLY, LAST)
-        products(3, EARLY, LAST)
-        products(2, LAST, C)
-        products(3, LAST, C)
+        products(0, 0, C, dy_edge[0][:])
+        products(1, 0, C, dy_edge[1][:])
+        products(2, 0, LAST, dy_edge[2][:, :LAST])
+        products(3, 0, EARLY, dy_last[:, :EARLY])
+        scalar_sums(0)
+        scalar_sums(1)
+        products(3, EARLY, LAST, dy_last[:, EARLY:LAST])
+        gather_dy(M_TILES - 1, dy_last[:, :P], LAST, C, SHORT_WINDOW)
+        products(2, LAST, C, dy_edge[2][:, LAST:])
+        products(3, LAST, C, dy_last[:, :P])
+        vector_sums(2)
         turn(0, 4)
-        store(nc.sync, 0, 0, EARLY)
-        vector_sums(2, 4)
-        vector_sums(3, 8)
+        store(nc.sync, 0, 512)
+        vector_sums(3)
         turn(4, 8)
-        store(nc.scalar, 4, EARLY, LAST)
+        store(nc.scalar, 512, LAST)
         turn(8, 9)
-        store(nc.sync, 8, LAST, C)
+        store(nc.sync, LAST, C)

@@ -23,7 +23,7 @@ DY_WINDOW = 1376
 SHORT_WINDOW = 704
 LAST = C - P
 EARLY = 512
-U_WINDOWS = (1040, 1040, 912, 528)
+U_WINDOWS = (1040, 1040, 528, 912)
 GROUPS = ((0, 256), (256, 512), (512, 896), (896, 1024))
 
 FLOPS = 2 * D * M * X
@@ -44,7 +44,7 @@ def tile_attend_gedgew_kernel(tc, W_words, W_scales, hT, dyT, soffs, toffs, out)
 
         dy_all = keep.tile([P, (M_TILES - 1) * X + DY_WINDOW], F32, name="dy_all")
         dy_col = [(M_TILES - 1 - j) * X for j in range(M_TILES)]
-        dy_edge = [keep.tile([P, C], F32, name="dy_edge%d" % j) for j in range(M_TILES - 1)]
+        dy_edge = [keep.tile([P, C if j < 2 else LAST], F32, name="dy_edge%d" % j) for j in range(M_TILES - 1)]
         w_scales = keep.tile([P, M], U8, name="w_scales", align_bytes=64)
         w_words = keep.tile([P, 2 * M], U8, name="w_words", align_bytes=64)
         h_raw = [keep.tile([P, PACK, HALF], F32, name="h_raw%d" % a, tag="h_raw%d" % a) for a in range(2)]
@@ -96,13 +96,14 @@ def tile_attend_gedgew_kernel(tc, W_words, W_scales, hT, dyT, soffs, toffs, out)
                 dst, dy_all[:, dy_col[j] : dy_col[j] + window].indirect(dst_list[:, c0 // STRIPE : c1 // STRIPE])
             )
 
-        for j in range(M_TILES - 1):
-            gather_dy(j, dy_edge[j][:], 0, C, DY_WINDOW)
+        gather_dy(0, dy_edge[0][:], 0, C, DY_WINDOW)
+        gather_dy(1, dy_edge[1][:], 0, C, DY_WINDOW)
+        gather_dy(2, dy_edge[2][:], 0, LAST, DY_WINDOW)
         nc.vector.quantize_mx(
             out=h_codes[:].bitcast(FP8X4), scales=h_scales[:], in_=h_bf[:].rearrange("p x t -> p (x t)")
         )
         dy_last = keep.tile([P, C], F32, name="dy_last", tag="h_raw1")
-        gather_dy(M_TILES - 1, dy_last[:, :LAST], 0, LAST, DY_WINDOW)
+        gather_dy(3, dy_last[:], 0, C, DY_WINDOW)
 
         for j in range(M_TILES):
             u_bank = psum.tile([P, X], F32, name="u_bank%d" % j, tag="bank%d" % j)
@@ -134,7 +135,7 @@ def tile_attend_gedgew_kernel(tc, W_words, W_scales, hT, dyT, soffs, toffs, out)
                     q[:, c - c0 : c - c0 + P],
                     ident[:],
                     start=(j == 0 and c == lo),
-                    stop=(j == M_TILES - 1 and c + P == hi),
+                    stop=(j == 2 and c + P == hi),
                     is_transpose=True,
                 )
 
@@ -173,14 +174,14 @@ def tile_attend_gedgew_kernel(tc, W_words, W_scales, hT, dyT, soffs, toffs, out)
 
         products(0, 0, C, dy_edge[0][:])
         products(1, 0, C, dy_edge[1][:])
-        products(2, 0, LAST, dy_edge[2][:, :LAST])
-        products(3, 0, EARLY, dy_last[:, :EARLY])
+        products(3, 0, LAST, dy_last[:, :LAST])
+        products(2, 0, EARLY, dy_edge[2][:, :EARLY])
         scalar_sums(0)
         scalar_sums(1)
-        products(3, EARLY, LAST, dy_last[:, EARLY:LAST])
-        gather_dy(M_TILES - 1, dy_last[:, :P], LAST, C, SHORT_WINDOW)
-        products(2, LAST, C, dy_edge[2][:, LAST:])
-        products(3, LAST, C, dy_last[:, :P])
+        products(2, EARLY, LAST, dy_edge[2][:, EARLY:LAST])
+        gather_dy(2, dy_edge[2][:, :P], LAST, C, SHORT_WINDOW)
+        products(3, LAST, C, dy_last[:, LAST:])
+        products(2, LAST, C, dy_edge[2][:, :P])
         vector_sums(2)
         turn(0, 4)
         store(nc.sync, 0, 512)

@@ -19,20 +19,20 @@ M_TILES = M // P
 HALF = X // 2
 STRIPE = 16
 BLOCK = 32
+BANKS = 8
 DY_WINDOW = 1376
-SHORT_WINDOW = 704
+EARLY = 768
 LAST = C - P
-EARLY = 512
-U_WINDOWS = (1040, 1040, 528, 912)
-GROUPS = ((0, 256), (256, 512), (512, 896), (896, 1024))
+U_WINDOWS = (C + STRIPE, C + STRIPE, EARLY + STRIPE, EARLY + STRIPE)
+GROUPS = ((0, 1), (1, 3), (3, 6), (6, 7), (7, 8))
+FIRST = 3
+N_BLOCKS = 9
 
 FLOPS = 2 * D * M * X
 
 
 def tile_attend_gedgew_kernel(tc, W_words, W_scales, hT, dyT, soffs, toffs, out):
     nc = tc.nc
-    mult = mybir.AluOpType.mult
-    add = mybir.AluOpType.add
 
     with ExitStack() as ctx:
         lists = ctx.enter_context(tc.tile_pool(name="lists", bufs=1))
@@ -41,10 +41,8 @@ def tile_attend_gedgew_kernel(tc, W_words, W_scales, hT, dyT, soffs, toffs, out)
 
         dst_list = lists.tile([P, C // STRIPE], U16, name="dst_list")
         src_list = lists.tile([P, C // STRIPE], U16, name="src_list")
-
         dy_all = keep.tile([P, (M_TILES - 1) * X + DY_WINDOW], F32, name="dy_all")
         dy_col = [(M_TILES - 1 - j) * X for j in range(M_TILES)]
-        dy_edge = [keep.tile([P, C if j < 2 else LAST], F32, name="dy_edge%d" % j) for j in range(M_TILES - 1)]
         w_scales = keep.tile([P, M], U8, name="w_scales", align_bytes=64)
         w_words = keep.tile([P, 2 * M], U8, name="w_words", align_bytes=64)
         h_raw = [keep.tile([P, PACK, HALF], F32, name="h_raw%d" % a, tag="h_raw%d" % a) for a in range(2)]
@@ -54,8 +52,8 @@ def tile_attend_gedgew_kernel(tc, W_words, W_scales, hT, dyT, soffs, toffs, out)
         u = [keep.tile([P, U_WINDOWS[j]], F32, name="u%d" % j) for j in range(M_TILES)]
         ident = keep.tile([P, P], F32, name="ident")
         zero = keep.tile([P, 1], F32, name="zero")
-        sums = keep.tile([P, 9 * BLOCK], F32, name="sums", align_bytes=64)
-        rows = keep.tile([P, 9 * BLOCK], F32, name="rows", align_bytes=64)
+        sums = keep.tile([P, N_BLOCKS * BLOCK], F32, name="sums", align_bytes=64)
+        rows = keep.tile([P, N_BLOCKS * BLOCK], F32, name="rows", align_bytes=64)
         scratch = keep.tile([P, C], F32, name="scratch")
 
         nc.vector.memset(zero[:], 0.0)
@@ -64,7 +62,7 @@ def tile_attend_gedgew_kernel(tc, W_words, W_scales, hT, dyT, soffs, toffs, out)
         make_identity(nc, ident[:])
         for j in range(M_TILES):
             nc.scalar.copy(out=u[j][:, X:], in_=zero[:].to_broadcast([P, U_WINDOWS[j] - X]))
-        nc.scalar.copy(out=sums[:], in_=zero[:].to_broadcast([P, 9 * BLOCK]))
+        nc.scalar.copy(out=sums[:], in_=zero[:].to_broadcast([P, N_BLOCKS * BLOCK]))
 
         def load_dy(j):
             nc.sync.dma_start(out=dy_all[:, dy_col[j] : dy_col[j] + X], in_=dyT[j * P : (j + 1) * P, :])
@@ -91,19 +89,16 @@ def tile_attend_gedgew_kernel(tc, W_words, W_scales, hT, dyT, soffs, toffs, out)
                 in_=h_raw[a][:].rearrange("p t (c i) -> p c t i", i=4),
             )
 
-        def gather_dy(j, dst, c0, c1, window):
-            nc.vector.tensor_copy(
-                dst, dy_all[:, dy_col[j] : dy_col[j] + window].indirect(dst_list[:, c0 // STRIPE : c1 // STRIPE])
-            )
+        def gather_dy(j, tag):
+            edge = keep.tile([P, C], F32, name="dy_edge%d" % j, tag=tag)
+            nc.vector.tensor_copy(edge[:], dy_all[:, dy_col[j] : dy_col[j] + DY_WINDOW].indirect(dst_list[:]))
+            return edge
 
-        gather_dy(0, dy_edge[0][:], 0, C, DY_WINDOW)
-        gather_dy(1, dy_edge[1][:], 0, C, DY_WINDOW)
-        gather_dy(2, dy_edge[2][:], 0, LAST, DY_WINDOW)
+        dy_edge = [gather_dy(j, "dy_edge%d" % j) for j in range(M_TILES - 1)]
         nc.vector.quantize_mx(
             out=h_codes[:].bitcast(FP8X4), scales=h_scales[:], in_=h_bf[:].rearrange("p x t -> p (x t)")
         )
-        dy_last = keep.tile([P, C], F32, name="dy_last", tag="h_raw1")
-        gather_dy(3, dy_last[:], 0, C, DY_WINDOW)
+        dy_edge.append(gather_dy(M_TILES - 1, "h_raw1"))
 
         for j in range(M_TILES):
             u_bank = psum.tile([P, X], F32, name="u_bank%d" % j, tag="bank%d" % j)
@@ -119,74 +114,80 @@ def tile_attend_gedgew_kernel(tc, W_words, W_scales, hT, dyT, soffs, toffs, out)
             nc.scalar.copy(out=u[j][:, :X], in_=u_bank[:])
 
         accs = [
-            psum.tile([P, c1 - c0], F32, name="acc%d" % g, tag="bank%d" % ((M_TILES + g) % 8))
-            for g, (c0, c1) in enumerate(GROUPS)
+            psum.tile([P, (k1 - k0) * P], F32, name="acc%d" % g, tag="bank%d" % ((M_TILES + g) % BANKS))
+            for g, (k0, k1) in enumerate(GROUPS)
         ]
-        group_of = {c: g for g, (c0, c1) in enumerate(GROUPS) for c in range(c0, c1, P)}
+        group_of = {k: g for g, (k0, k1) in enumerate(GROUPS) for k in range(k0, k1)}
 
-        def products(j, c0, c1, dy):
+        def products(j, c0, c1):
             q = keep.tile([P, c1 - c0], F32, name="q%d_%d" % (j, c0))
-            nc.vector.tensor_tensor(q[:], u[j][:].indirect(src_list[:, c0 // STRIPE : c1 // STRIPE]), dy, mult)
-            for c in range(c0, c1, P):
-                g = group_of[c]
-                lo, hi = GROUPS[g]
+            nc.vector.tensor_tensor(
+                q[:],
+                u[j][:].indirect(src_list[:, c0 // STRIPE : c1 // STRIPE]),
+                dy_edge[j][:, c0:c1],
+                mybir.AluOpType.mult,
+            )
+            for k in range(c0 // P, c1 // P):
+                k0, k1 = GROUPS[group_of[k]]
                 nc.tensor.matmul(
-                    accs[g][:, c - lo : c - lo + P],
-                    q[:, c - c0 : c - c0 + P],
+                    accs[group_of[k]][:, (k - k0) * P : (k - k0 + 1) * P],
+                    q[:, k * P - c0 : (k + 1) * P - c0],
                     ident[:],
-                    start=(j == 0 and c == lo),
-                    stop=(j == 2 and c + P == hi),
+                    start=(j == 0 and k == k0),
+                    stop=(j == M_TILES - 1 and k + 1 == k1),
                     is_transpose=True,
                 )
 
-        def block_of(c):
-            return c // P if c < LAST else 8
+        def block_of(k):
+            if k < FIRST:
+                return k
+            return 4 + k - FIRST if k < LAST // P else N_BLOCKS - 1
 
         def scalar_sums(g):
-            lo, hi = GROUPS[g]
-            for c in range(lo, hi, P):
+            k0, k1 = GROUPS[g]
+            for k in range(k0, k1):
                 nc.scalar.activation(
-                    out=scratch[:, c : c + P],
-                    in_=accs[g][:, c - lo : c - lo + P],
+                    out=scratch[:, k * P : (k + 1) * P],
+                    in_=accs[g][:, (k - k0) * P : (k - k0 + 1) * P],
                     func=mybir.ActivationFunctionType.Copy,
-                    accum_out=sums[:, block_of(c) * BLOCK : block_of(c) * BLOCK + 1],
+                    accum_out=sums[:, block_of(k) * BLOCK : block_of(k) * BLOCK + 1],
                 )
 
         def vector_sums(g):
-            lo, hi = GROUPS[g]
+            k0, k1 = GROUPS[g]
             nc.vector.tensor_reduce(
-                out=sums[:, block_of(lo) * BLOCK : (block_of(lo) + (hi - lo) // P) * BLOCK : BLOCK],
+                out=sums[:, block_of(k0) * BLOCK : (block_of(k0) + k1 - k0) * BLOCK : BLOCK],
                 in_=accs[g][:].rearrange("p (k m) -> p k m", m=P),
                 axis=mybir.AxisListType.X,
-                op=add,
+                op=mybir.AluOpType.add,
             )
 
         def turn(b0, b1):
             cols = slice(b0 * BLOCK, b1 * BLOCK)
             nc.vector.transpose(rows[:, cols], sums[:, cols])
 
-        def store(queue, c0, c1):
-            b0 = block_of(c0)
+        def store(queue, k0, k1):
+            b0 = block_of(k0)
             queue.dma_start(
-                out=out[:, c0:c1].rearrange("o (j b q) -> b (o j) q", b=P // BLOCK, q=BLOCK),
-                in_=rows[0:P:BLOCK, b0 * BLOCK : (b0 + (c1 - c0) // P) * BLOCK].rearrange("b (j q) -> b j q", q=BLOCK),
+                out=out[:, k0 * P : k1 * P].rearrange("o (j b q) -> b (o j) q", b=P // BLOCK, q=BLOCK),
+                in_=rows[0:P:BLOCK, b0 * BLOCK : (b0 + k1 - k0) * BLOCK].rearrange("b (j q) -> b j q", q=BLOCK),
             )
 
-        products(0, 0, C, dy_edge[0][:])
-        products(1, 0, C, dy_edge[1][:])
-        products(3, 0, LAST, dy_last[:, :LAST])
-        products(2, 0, EARLY, dy_edge[2][:, :EARLY])
+        products(0, 0, C)
+        products(1, 0, C)
+        products(2, 0, EARLY)
+        products(3, 0, EARLY)
         scalar_sums(0)
         scalar_sums(1)
-        products(2, EARLY, LAST, dy_edge[2][:, EARLY:LAST])
-        gather_dy(2, dy_edge[2][:, :P], LAST, C, SHORT_WINDOW)
-        products(3, LAST, C, dy_last[:, LAST:])
-        products(2, LAST, C, dy_edge[2][:, :P])
+        products(2, EARLY, C)
+        products(3, EARLY, LAST)
+        products(3, LAST, C)
         vector_sums(2)
-        turn(0, 4)
-        store(nc.sync, 0, 512)
         vector_sums(3)
+        turn(0, 4)
+        store(nc.sync, 0, FIRST)
+        vector_sums(4)
         turn(4, 8)
-        store(nc.scalar, 512, LAST)
+        store(nc.scalar, FIRST, 7)
         turn(8, 9)
-        store(nc.sync, LAST, C)
+        store(nc.sync, 7, 8)

@@ -21,11 +21,11 @@ STRIPE = 16
 BLOCK = 32
 BANKS = 8
 DY_WINDOW = 1376
-EARLY = 768
 LAST = C - P
-U_WINDOWS = (C + STRIPE, C + STRIPE, EARLY + STRIPE, EARLY + STRIPE)
-GROUPS = ((0, 1), (1, 3), (3, 6), (6, 7), (7, 8))
-FIRST = 3
+PIECES = ((0, 0, C), (1, 0, C), (2, 0, 512), (3, 0, 768), (2, 512, LAST), (3, 768, C), (2, LAST, C))
+U_WINDOWS = [max(X, max(c1 - c0 for t, c0, c1 in PIECES if t == j)) + STRIPE for j in range(M_TILES)]
+GROUPS = ((0, 2), (2, 4), (4, 6), (6, 7), (7, 8))
+FIRST = 4
 N_BLOCKS = 9
 
 FLOPS = 2 * D * M * X
@@ -119,7 +119,10 @@ def tile_attend_gedgew_kernel(tc, W_words, W_scales, hT, dyT, soffs, toffs, out)
         ]
         group_of = {k: g for g, (k0, k1) in enumerate(GROUPS) for k in range(k0, k1)}
 
-        def products(j, c0, c1):
+        closer = {k: n for n, (j, c0, c1) in enumerate(PIECES) for k in range(c0 // P, c1 // P)}
+
+        def products(n):
+            j, c0, c1 = PIECES[n]
             q = keep.tile([P, c1 - c0], F32, name="q%d_%d" % (j, c0))
             nc.vector.tensor_tensor(
                 q[:],
@@ -134,7 +137,7 @@ def tile_attend_gedgew_kernel(tc, W_words, W_scales, hT, dyT, soffs, toffs, out)
                     q[:, k * P - c0 : (k + 1) * P - c0],
                     ident[:],
                     start=(j == 0 and k == k0),
-                    stop=(j == M_TILES - 1 and k + 1 == k1),
+                    stop=(n == closer[k] and k + 1 == k1),
                     is_transpose=True,
                 )
 
@@ -173,15 +176,15 @@ def tile_attend_gedgew_kernel(tc, W_words, W_scales, hT, dyT, soffs, toffs, out)
                 in_=rows[0:P:BLOCK, b0 * BLOCK : (b0 + k1 - k0) * BLOCK].rearrange("b (j q) -> b j q", q=BLOCK),
             )
 
-        products(0, 0, C)
-        products(1, 0, C)
-        products(2, 0, EARLY)
-        products(3, 0, EARLY)
+        products(0)
+        products(1)
+        products(2)
+        products(3)
         scalar_sums(0)
         scalar_sums(1)
-        products(2, EARLY, C)
-        products(3, EARLY, LAST)
-        products(3, LAST, C)
+        products(4)
+        products(5)
+        products(6)
         vector_sums(2)
         vector_sums(3)
         turn(0, 4)

@@ -71,9 +71,9 @@ def tile_attend_gedgew_kernel(tc, W_words, W_scales, hT, dyT, soffs, toffs, out)
         load_dy(0)
         nc.sync.dma_start(dst_list[:], toffs)
         load_dy(1)
+        load_dy(2)
         for a in range(2):
             nc.sync.dma_start(out=h_raw[a][:], in_=h_rows[:, :, a * HALF : (a + 1) * HALF])
-        load_dy(2)
         nc.sync.dma_start(out=w_words[:].bitcast(I32), in_=W_words[0].bitcast(I32))
         for quad in range(4):
             nc.sync.dma_start(

@@ -76,7 +76,8 @@ def tile_attend_gedgew_kernel(tc, W_words, W_scales, hT, dyT, soffs, toffs, out)
             nc.sync.dma_start(out=h_raw[a][:], in_=h_rows[:, :, a * HALF : (a + 1) * HALF])
         nc.sync.dma_start(out=w_words[:].bitcast(I32), in_=W_words[0].bitcast(I32))
         for quad in range(4):
-            nc.sync.dma_start(
+            queue = nc.scalar if quad == 0 else nc.sync
+            queue.dma_start(
                 out=w_scales[32 * quad : 32 * quad + 4, :].bitcast(I32),
                 in_=W_scales[0, 4 * quad : 4 * quad + 4, :].bitcast(I32),
             )

@@ -20,10 +20,11 @@ HALF = X // 2
 STRIPE = 16
 BLOCK = 32
 BANKS = 8
-DY_WINDOW = 1376
 LAST = C - P
 PIECES = ((0, 0, C), (1, 0, C), (2, 0, 512), (3, 0, 768), (2, 512, LAST), (3, 768, C), (2, LAST, C))
 U_WINDOWS = [max(X, max(c1 - c0 for t, c0, c1 in PIECES if t == j)) + STRIPE for j in range(M_TILES)]
+DY_PIECES = ((0, 0, C), (1, 0, C), (2, 0, 512), (3, 0, 768), (2, 512, C), (3, 768, C))
+DY_WINDOWS = [max(X, max(c1 - c0 for t, c0, c1 in DY_PIECES if t == j)) + STRIPE for j in range(M_TILES)]
 GROUPS = ((0, 2), (2, 4), (4, 6), (6, 7), (7, 8))
 FIRST = 4
 N_BLOCKS = 9
@@ -41,8 +42,8 @@ def tile_attend_gedgew_kernel(tc, W_words, W_scales, hT, dyT, soffs, toffs, out)
 
         dst_list = lists.tile([P, C // STRIPE], U16, name="dst_list")
         src_list = lists.tile([P, C // STRIPE], U16, name="src_list")
-        dy_all = keep.tile([P, (M_TILES - 1) * X + DY_WINDOW], F32, name="dy_all")
-        dy_col = [(M_TILES - 1 - j) * X for j in range(M_TILES)]
+        dy = [keep.tile([P, DY_WINDOWS[j]], F32, name="dy%d" % j) for j in range(M_TILES)]
+        dy_edge = [keep.tile([P, C], F32, name="dy_edge%d" % j) for j in range(M_TILES)]
         w_scales = keep.tile([P, M], U8, name="w_scales", align_bytes=64)
         w_words = keep.tile([P, 2 * M], U8, name="w_words", align_bytes=64)
         h_raw = [keep.tile([P, PACK, HALF], F32, name="h_raw%d" % a, tag="h_raw%d" % a) for a in range(2)]
@@ -57,49 +58,54 @@ def tile_attend_gedgew_kernel(tc, W_words, W_scales, hT, dyT, soffs, toffs, out)
         scratch = keep.tile([P, C], F32, name="scratch")
 
         nc.vector.memset(zero[:], 0.0)
-        nc.vector.memset(dy_all[:, M_TILES * X :], 0.0)
         nc.vector.memset(w_scales[:].bitcast(I32), 0)
+        for j in range(M_TILES):
+            nc.vector.memset(dy[j][:, X:], 0.0)
         make_identity(nc, ident[:])
         for j in range(M_TILES):
-            nc.scalar.copy(out=u[j][:, X:], in_=zero[:].to_broadcast([P, U_WINDOWS[j] - X]))
+            nc.vector.memset(u[j][:, X:], 0.0)
         nc.scalar.copy(out=sums[:], in_=zero[:].to_broadcast([P, N_BLOCKS * BLOCK]))
 
         def load_dy(j):
-            nc.sync.dma_start(out=dy_all[:, dy_col[j] : dy_col[j] + X], in_=dyT[j * P : (j + 1) * P, :])
+            nc.sync.dma_start(out=dy[j][:, :X], in_=dyT[j * P : (j + 1) * P, :])
 
         h_rows = hT.rearrange("(p t) x -> p t x", t=PACK)
         load_dy(0)
         nc.sync.dma_start(dst_list[:], toffs)
-        load_dy(1)
-        load_dy(2)
         for a in range(2):
             nc.sync.dma_start(out=h_raw[a][:], in_=h_rows[:, :, a * HALF : (a + 1) * HALF])
         nc.sync.dma_start(out=w_words[:].bitcast(I32), in_=W_words[0].bitcast(I32))
         for quad in range(4):
-            queue = nc.scalar if quad == 0 else nc.sync
-            queue.dma_start(
+            nc.sync.dma_start(
                 out=w_scales[32 * quad : 32 * quad + 4, :].bitcast(I32),
                 in_=W_scales[0, 4 * quad : 4 * quad + 4, :].bitcast(I32),
             )
-        load_dy(3)
+        load_dy(1)
         nc.sync.dma_start(src_list[:], soffs)
+        load_dy(2)
+        load_dy(3)
 
-        for a in range(2):
-            nc.scalar.copy(
-                out=h_bf[:, a * HALF : (a + 1) * HALF, :].rearrange("p (c i) t -> p c t i", i=4),
-                in_=h_raw[a][:].rearrange("p t (c i) -> p c t i", i=4),
+        def gather_dy(n):
+            j, c0, c1 = DY_PIECES[n]
+            nc.scalar.activation(
+                out=dy_edge[j][:, c0:c1],
+                in_=dy[j][:].indirect(dst_list[:, c0 // STRIPE : c1 // STRIPE]),
+                func=mybir.ActivationFunctionType.Copy,
             )
 
-        def gather_dy(j, tag):
-            edge = keep.tile([P, C], F32, name="dy_edge%d" % j, tag=tag)
-            nc.vector.tensor_copy(edge[:], dy_all[:, dy_col[j] : dy_col[j] + DY_WINDOW].indirect(dst_list[:]))
-            return edge
-
-        dy_edge = [gather_dy(j, "dy_edge%d" % j) for j in range(M_TILES - 1)]
-        nc.vector.quantize_mx(
-            out=h_codes[:].bitcast(FP8X4), scales=h_scales[:], in_=h_bf[:].rearrange("p x t -> p (x t)")
-        )
-        dy_edge.append(gather_dy(M_TILES - 1, "h_raw1"))
+        gather_dy(0)
+        for a in range(2):
+            nodes = slice(a * HALF, (a + 1) * HALF)
+            nc.vector.tensor_copy(
+                out=h_bf[:, nodes, :].rearrange("p (c i) t -> p c t i", i=4),
+                in_=h_raw[a][:].rearrange("p t (c i) -> p c t i", i=4),
+            )
+            nc.vector.quantize_mx(
+                out=h_codes[:, nodes].bitcast(FP8X4),
+                scales=h_scales[:, nodes],
+                in_=h_bf[:, nodes, :].rearrange("p x t -> p (x t)"),
+            )
+        gather_dy(1)
 
         for j in range(M_TILES):
             u_bank = psum.tile([P, X], F32, name="u_bank%d" % j, tag="bank%d" % j)
@@ -112,7 +118,12 @@ def tile_attend_gedgew_kernel(tc, W_words, W_scales, hT, dyT, soffs, toffs, out)
                 start=True,
                 stop=True,
             )
-            nc.scalar.copy(out=u[j][:, :X], in_=u_bank[:])
+            if j == 0:
+                nc.vector.tensor_copy(out=u[j][:, :X], in_=u_bank[:])
+            else:
+                nc.scalar.copy(out=u[j][:, :X], in_=u_bank[:])
+        for n in range(2, len(DY_PIECES)):
+            gather_dy(n)
 
         accs = [
             psum.tile([P, (k1 - k0) * P], F32, name="acc%d" % g, tag="bank%d" % ((M_TILES + g) % BANKS))

@@ -21,9 +21,10 @@ STRIPE = 16
 BLOCK = 32
 BANKS = 8
 LAST = C - P
-PIECES = ((0, 0, C), (1, 0, C), (2, 0, 512), (3, 0, 768), (2, 512, LAST), (3, 768, C), (2, LAST, C))
+PIECES = ((0, 0, C), (1, 0, C), (2, 0, 512), (3, 0, 512), (3, 512, C), (2, 512, 768), (2, 768, LAST), (2, LAST, C))
+PLAIN = (3, 512, C)
 U_WINDOWS = [max(X, max(c1 - c0 for t, c0, c1 in PIECES if t == j)) + STRIPE for j in range(M_TILES)]
-DY_PIECES = ((0, 0, C), (1, 0, C), (2, 0, 512), (3, 0, 768), (2, 512, C), (3, 768, C))
+DY_PIECES = ((0, 0, C), (1, 0, C), (2, 0, 512), (3, 0, 512), (3, 512, C), (2, 512, 768), (2, 768, C))
 DY_WINDOWS = [max(X, max(c1 - c0 for t, c0, c1 in DY_PIECES if t == j)) + STRIPE for j in range(M_TILES)]
 GROUPS = ((0, 2), (2, 4), (4, 6), (6, 7), (7, 8))
 FIRST = 4
@@ -63,23 +64,30 @@ def tile_attend_gedgew_kernel(tc, W_words, W_scales, hT, dyT, soffs, toffs, out)
             nc.vector.memset(dy[j][:, X:], 0.0)
         make_identity(nc, ident[:])
         for j in range(M_TILES):
-            nc.vector.memset(u[j][:, X:], 0.0)
+            nc.gpsimd.memset(u[j][:, X:], 0.0)
         nc.scalar.copy(out=sums[:], in_=zero[:].to_broadcast([P, N_BLOCKS * BLOCK]))
 
         def load_dy(j):
             nc.sync.dma_start(out=dy[j][:, :X], in_=dyT[j * P : (j + 1) * P, :])
 
         h_rows = hT.rearrange("(p t) x -> p t x", t=PACK)
-        load_dy(0)
-        nc.sync.dma_start(dst_list[:], toffs)
-        for a in range(2):
+
+        def load_h(a):
             nc.sync.dma_start(out=h_raw[a][:], in_=h_rows[:, :, a * HALF : (a + 1) * HALF])
-        nc.sync.dma_start(out=w_words[:].bitcast(I32), in_=W_words[0].bitcast(I32))
-        for quad in range(4):
+
+        def load_scales(quad):
             nc.sync.dma_start(
                 out=w_scales[32 * quad : 32 * quad + 4, :].bitcast(I32),
                 in_=W_scales[0, 4 * quad : 4 * quad + 4, :].bitcast(I32),
             )
+
+        load_dy(0)
+        nc.sync.dma_start(dst_list[:], toffs)
+        load_h(0)
+        for quad in range(4):
+            load_scales(quad)
+        load_h(1)
+        nc.sync.dma_start(out=w_words[:].bitcast(I32), in_=W_words[0].bitcast(I32))
         load_dy(1)
         nc.sync.dma_start(src_list[:], soffs)
         load_dy(2)
@@ -93,40 +101,65 @@ def tile_attend_gedgew_kernel(tc, W_words, W_scales, hT, dyT, soffs, toffs, out)
                 func=mybir.ActivationFunctionType.Copy,
             )
 
-        gather_dy(0)
-        for a in range(2):
-            nodes = slice(a * HALF, (a + 1) * HALF)
+        def cast(x0, x1):
+            a = x0 // HALF
             nc.vector.tensor_copy(
-                out=h_bf[:, nodes, :].rearrange("p (c i) t -> p c t i", i=4),
-                in_=h_raw[a][:].rearrange("p t (c i) -> p c t i", i=4),
+                out=h_bf[:, x0:x1, :].rearrange("p (c i) t -> p c t i", i=4),
+                in_=h_raw[a][:, :, x0 - a * HALF : x1 - a * HALF].rearrange("p t (c i) -> p c t i", i=4),
             )
-            nc.vector.quantize_mx(
-                out=h_codes[:, nodes].bitcast(FP8X4),
-                scales=h_scales[:, nodes],
-                in_=h_bf[:, nodes, :].rearrange("p x t -> p (x t)"),
-            )
-        gather_dy(1)
 
-        for j in range(M_TILES):
-            u_bank = psum.tile([P, X], F32, name="u_bank%d" % j, tag="bank%d" % j)
+        def quantise(x0, x1):
+            nc.vector.quantize_mx(
+                out=h_codes[:, x0:x1].bitcast(FP8X4),
+                scales=h_scales[:, x0:x1],
+                in_=h_bf[:, x0:x1, :].rearrange("p x t -> p (x t)"),
+            )
+
+        def multiply(j, bank, x0, x1, at):
             nc.tensor.matmul_mx(
-                out=u_bank[:],
+                out=bank[:, at : at + x1 - x0],
                 lhsT=w_words[:, 2 * P * j : 2 * P * (j + 1)].bitcast(FP4X4),
                 lhsT_scale=w_scales[:, P * j : P * (j + 1)],
-                rhs=h_codes[:].bitcast(FP8X4),
-                rhs_scale=h_scales[:],
+                rhs=h_codes[:, x0:x1].bitcast(FP8X4),
+                rhs_scale=h_scales[:, x0:x1],
                 start=True,
                 stop=True,
             )
-            if j == 0:
-                nc.vector.tensor_copy(out=u[j][:, :X], in_=u_bank[:])
-            else:
-                nc.scalar.copy(out=u[j][:, :X], in_=u_bank[:])
-        for n in range(2, len(DY_PIECES)):
-            gather_dy(n)
+
+        def make_u(j, x0, x1, b, copy, step=None):
+            bank = psum.tile([P, x1 - x0], F32, name="u_bank%d" % b, tag="bank%d" % b)
+            for x in range(x0, x1, step or x1 - x0):
+                multiply(j, bank, x, x + (step or x1 - x0), x - x0)
+            copy(out=u[j][:, x0:x1], in_=bank[:])
+
+        gather_dy(0)
+        cast(0, HALF)
+        quantise(0, HALF)
+        cast(HALF, HALF + P)
+        cast(HALF + P, X)
+        quantise(HALF, HALF + P)
+        quantise(HALF + P, X)
+        make_u(0, 0, HALF, 0, nc.vector.tensor_copy)
+        make_u(1, 0, HALF, 5, nc.vector.tensor_copy)
+        make_u(0, HALF, X, 1, nc.vector.tensor_copy, P)
+        gather_dy(1)
+        make_u(1, HALF, X, 2, nc.scalar.copy)
+        make_u(2, 0, X, 3, nc.scalar.copy)
+        gather_dy(2)
+        make_u(3, 0, X, 4, nc.scalar.copy)
+        gather_dy(3)
+        gather_dy(4)
+        u_edge = keep.tile([P, PLAIN[2] - PLAIN[1]], F32, name="u_edge")
+        nc.scalar.activation(
+            out=u_edge[:],
+            in_=u[PLAIN[0]][:].indirect(src_list[:, PLAIN[1] // STRIPE : PLAIN[2] // STRIPE]),
+            func=mybir.ActivationFunctionType.Copy,
+        )
+        gather_dy(5)
+        gather_dy(6)
 
         accs = [
-            psum.tile([P, (k1 - k0) * P], F32, name="acc%d" % g, tag="bank%d" % ((M_TILES + g) % BANKS))
+            psum.tile([P, (k1 - k0) * P], F32, name="acc%d" % g, tag="bank%d" % ((M_TILES + 2 + g) % BANKS))
             for g, (k0, k1) in enumerate(GROUPS)
         ]
         group_of = {k: g for g, (k0, k1) in enumerate(GROUPS) for k in range(k0, k1)}
@@ -138,7 +171,7 @@ def tile_attend_gedgew_kernel(tc, W_words, W_scales, hT, dyT, soffs, toffs, out)
             q = keep.tile([P, c1 - c0], F32, name="q%d_%d" % (j, c0))
             nc.vector.tensor_tensor(
                 q[:],
-                u[j][:].indirect(src_list[:, c0 // STRIPE : c1 // STRIPE]),
+                u_edge[:] if PIECES[n] == PLAIN else u[j][:].indirect(src_list[:, c0 // STRIPE : c1 // STRIPE]),
                 dy_edge[j][:, c0:c1],
                 mybir.AluOpType.mult,
             )
@@ -196,8 +229,9 @@ def tile_attend_gedgew_kernel(tc, W_words, W_scales, hT, dyT, soffs, toffs, out)
         scalar_sums(1)
         products(4)
         products(5)
+        scalar_sums(2)
         products(6)
-        vector_sums(2)
+        products(7)
         vector_sums(3)
         turn(0, 4)
         store(nc.sync, 0, FIRST)

@@ -229,12 +229,12 @@ def tile_attend_gedgew_kernel(tc, W_words, W_scales, hT, dyT, soffs, toffs, out)
         scalar_sums(1)
         products(4)
         products(5)
-        scalar_sums(2)
         products(6)
         products(7)
-        vector_sums(3)
         turn(0, 4)
         store(nc.sync, 0, FIRST)
+        vector_sums(2)
+        vector_sums(3)
         vector_sums(4)
         turn(4, 8)
         store(nc.scalar, FIRST, 7)

from contextlib import ExitStack

import concourse.mybir as mybir
from concourse.masks import make_identity

F32 = mybir.dt.float32
BF16 = mybir.dt.bfloat16
I32 = mybir.dt.int32
U32 = mybir.dt.uint32
U16 = mybir.dt.uint16
U8 = mybir.dt.uint8
FP8X4 = mybir.dt.float8_e4m3fn_x4
FP4X4 = mybir.dt.float4_e2m1fn_x4

P = 128
PACK = 4
D, M, X, C = 512, 512, 512, 1024
M_TILES = M // P
HALF = X // 2
STRIPE = 16
BLOCK = 32
BANKS = 8
LAST = C - P
PIECES = ((0, 0, C), (1, 0, C), (2, 0, 512), (3, 0, 512), (3, 512, C), (2, 512, 768), (2, 768, LAST), (2, LAST, C))
PLAIN = (3, 512, C)
U_WINDOWS = [max(X, max(c1 - c0 for t, c0, c1 in PIECES if t == j)) + STRIPE for j in range(M_TILES)]
DY_PIECES = ((0, 0, C), (1, 0, C), (2, 0, 512), (3, 0, 512), (3, 512, C), (2, 512, 768), (2, 768, C))
DY_WINDOWS = [max(X, max(c1 - c0 for t, c0, c1 in DY_PIECES if t == j)) + STRIPE for j in range(M_TILES)]
GROUPS = ((0, 2), (2, 4), (4, 6), (6, 7), (7, 8))
FIRST = 4
N_BLOCKS = 9

FLOPS = 2 * D * M * X


def tile_attend_gedgew_kernel(tc, W_words, W_scales, hT, dyT, soffs, toffs, out):
    nc = tc.nc

    with ExitStack() as ctx:
        lists = ctx.enter_context(tc.tile_pool(name="lists", bufs=1))
        keep = ctx.enter_context(tc.tile_pool(name="keep", bufs=1))
        psum = ctx.enter_context(tc.psum_pool(name="psum", bufs=1))

        dst_list = lists.tile([P, C // STRIPE], U16, name="dst_list")
        src_list = lists.tile([P, C // STRIPE], U16, name="src_list")
        dy = [keep.tile([P, DY_WINDOWS[j]], F32, name="dy%d" % j) for j in range(M_TILES)]
        dy_edge = [keep.tile([P, C], F32, name="dy_edge%d" % j) for j in range(M_TILES)]
        w_scales = keep.tile([P, M], U8, name="w_scales", align_bytes=64)
        w_words = keep.tile([P, 2 * M], U8, name="w_words", align_bytes=64)
        h_raw = [keep.tile([P, PACK, HALF], F32, name="h_raw%d" % a, tag="h_raw%d" % a) for a in range(2)]
        h_bf = keep.tile([P, X, PACK], BF16, name="h_bf", align_bytes=64)
        h_codes = keep.tile([P, X], U32, name="h_codes", align_bytes=64)
        h_scales = keep.tile([P, X], U8, name="h_scales", align_bytes=64)
        u = [keep.tile([P, U_WINDOWS[j]], F32, name="u%d" % j) for j in range(M_TILES)]
        ident = keep.tile([P, P], F32, name="ident")
        zero = keep.tile([P, 1], F32, name="zero")
        sums = keep.tile([P, N_BLOCKS * BLOCK], F32, name="sums", align_bytes=64)
        rows = keep.tile([P, N_BLOCKS * BLOCK], F32, name="rows", align_bytes=64)
        scratch = keep.tile([P, C], F32, name="scratch")

        nc.vector.memset(zero[:], 0.0)
        nc.vector.memset(w_scales[:].bitcast(I32), 0)
        for j in range(M_TILES):
            nc.vector.memset(dy[j][:, X:], 0.0)
        make_identity(nc, ident[:])
        for j in range(M_TILES):
            nc.gpsimd.memset(u[j][:, X:], 0.0)
        nc.scalar.copy(out=sums[:], in_=zero[:].to_broadcast([P, N_BLOCKS * BLOCK]))

        def load_dy(j):
            nc.sync.dma_start(out=dy[j][:, :X], in_=dyT[j * P : (j + 1) * P, :])

        h_rows = hT.rearrange("(p t) x -> p t x", t=PACK)

        def load_h(a):
            nc.sync.dma_start(out=h_raw[a][:], in_=h_rows[:, :, a * HALF : (a + 1) * HALF])

        def load_scales(quad):
            nc.sync.dma_start(
                out=w_scales[32 * quad : 32 * quad + 4, :].bitcast(I32),
                in_=W_scales[0, 4 * quad : 4 * quad + 4, :].bitcast(I32),
            )

        load_dy(0)
        nc.sync.dma_start(dst_list[:], toffs)
        load_h(0)
        for quad in range(4):
            load_scales(quad)
        load_h(1)
        nc.sync.dma_start(out=w_words[:].bitcast(I32), in_=W_words[0].bitcast(I32))
        load_dy(1)
        nc.sync.dma_start(src_list[:], soffs)
        load_dy(2)
        load_dy(3)

        def gather_dy(n):
            j, c0, c1 = DY_PIECES[n]
            nc.scalar.activation(
                out=dy_edge[j][:, c0:c1],
                in_=dy[j][:].indirect(dst_list[:, c0 // STRIPE : c1 // STRIPE]),
                func=mybir.ActivationFunctionType.Copy,
            )

        def cast(x0, x1):
            a = x0 // HALF
            nc.vector.tensor_copy(
                out=h_bf[:, x0:x1, :].rearrange("p (c i) t -> p c t i", i=4),
                in_=h_raw[a][:, :, x0 - a * HALF : x1 - a * HALF].rearrange("p t (c i) -> p c t i", i=4),
            )

        def quantise(x0, x1):
            nc.vector.quantize_mx(
                out=h_codes[:, x0:x1].bitcast(FP8X4),
                scales=h_scales[:, x0:x1],
                in_=h_bf[:, x0:x1, :].rearrange("p x t -> p (x t)"),
            )

        def multiply(j, bank, x0, x1, at):
            nc.tensor.matmul_mx(
                out=bank[:, at : at + x1 - x0],
                lhsT=w_words[:, 2 * P * j : 2 * P * (j + 1)].bitcast(FP4X4),
                lhsT_scale=w_scales[:, P * j : P * (j + 1)],
                rhs=h_codes[:, x0:x1].bitcast(FP8X4),
                rhs_scale=h_scales[:, x0:x1],
                start=True,
                stop=True,
            )

        def make_u(j, x0, x1, b, copy, step=None):
            bank = psum.tile([P, x1 - x0], F32, name="u_bank%d" % b, tag="bank%d" % b)
            for x in range(x0, x1, step or x1 - x0):
                multiply(j, bank, x, x + (step or x1 - x0), x - x0)
            copy(out=u[j][:, x0:x1], in_=bank[:])

        gather_dy(0)
        cast(0, HALF)
        quantise(0, HALF)
        cast(HALF, HALF + P)
        cast(HALF + P, X)
        quantise(HALF, HALF + P)
        quantise(HALF + P, X)
        make_u(0, 0, HALF, 0, nc.vector.tensor_copy)
        make_u(1, 0, HALF, 5, nc.vector.tensor_copy)
        make_u(0, HALF, X, 1, nc.vector.tensor_copy, P)
        gather_dy(1)
        make_u(1, HALF, X, 2, nc.scalar.copy)
        make_u(2, 0, X, 3, nc.scalar.copy)
        gather_dy(2)
        make_u(3, 0, X, 4, nc.scalar.copy)
        gather_dy(3)
        gather_dy(4)
        u_edge = keep.tile([P, PLAIN[2] - PLAIN[1]], F32, name="u_edge")
        nc.scalar.activation(
            out=u_edge[:],
            in_=u[PLAIN[0]][:].indirect(src_list[:, PLAIN[1] // STRIPE : PLAIN[2] // STRIPE]),
            func=mybir.ActivationFunctionType.Copy,
        )
        gather_dy(5)
        gather_dy(6)

        accs = [
            psum.tile([P, (k1 - k0) * P], F32, name="acc%d" % g, tag="bank%d" % ((M_TILES + 2 + g) % BANKS))
            for g, (k0, k1) in enumerate(GROUPS)
        ]
        group_of = {k: g for g, (k0, k1) in enumerate(GROUPS) for k in range(k0, k1)}

        closer = {k: n for n, (j, c0, c1) in enumerate(PIECES) for k in range(c0 // P, c1 // P)}

        def products(n):
            j, c0, c1 = PIECES[n]
            q = keep.tile([P, c1 - c0], F32, name="q%d_%d" % (j, c0))
            nc.vector.tensor_tensor(
                q[:],
                u_edge[:] if PIECES[n] == PLAIN else u[j][:].indirect(src_list[:, c0 // STRIPE : c1 // STRIPE]),
                dy_edge[j][:, c0:c1],
                mybir.AluOpType.mult,
            )
            for k in range(c0 // P, c1 // P):
                k0, k1 = GROUPS[group_of[k]]
                nc.tensor.matmul(
                    accs[group_of[k]][:, (k - k0) * P : (k - k0 + 1) * P],
                    q[:, k * P - c0 : (k + 1) * P - c0],
                    ident[:],
                    start=(j == 0 and k == k0),
                    stop=(n == closer[k] and k + 1 == k1),
                    is_transpose=True,
                )

        def block_of(k):
            if k < FIRST:
                return k
            return 4 + k - FIRST if k < LAST // P else N_BLOCKS - 1

        def scalar_sums(g):
            k0, k1 = GROUPS[g]
            for k in range(k0, k1):
                nc.scalar.activation(
                    out=scratch[:, k * P : (k + 1) * P],
                    in_=accs[g][:, (k - k0) * P : (k - k0 + 1) * P],
                    func=mybir.ActivationFunctionType.Copy,
                    accum_out=sums[:, block_of(k) * BLOCK : block_of(k) * BLOCK + 1],
                )

        def vector_sums(g):
            k0, k1 = GROUPS[g]
            nc.vector.tensor_reduce(
                out=sums[:, block_of(k0) * BLOCK : (block_of(k0) + k1 - k0) * BLOCK : BLOCK],
                in_=accs[g][:].rearrange("p (k m) -> p k m", m=P),
                axis=mybir.AxisListType.X,
                op=mybir.AluOpType.add,
            )

        def turn(b0, b1):
            cols = slice(b0 * BLOCK, b1 * BLOCK)
            nc.vector.transpose(rows[:, cols], sums[:, cols])

        def store(queue, k0, k1):
            b0 = block_of(k0)
            queue.dma_start(
                out=out[:, k0 * P : k1 * P].rearrange("o (j b q) -> b (o j) q", b=P // BLOCK, q=BLOCK),
                in_=rows[0:P:BLOCK, b0 * BLOCK : (b0 + k1 - k0) * BLOCK].rearrange("b (j q) -> b j q", q=BLOCK),
            )

        products(0)
        products(1)
        products(2)
        products(3)
        scalar_sums(0)
        scalar_sums(1)
        products(4)
        products(5)
        products(6)
        products(7)
        turn(0, 4)
        store(nc.sync, 0, FIRST)
        vector_sums(2)
        vector_sums(3)
        vector_sums(4)
        turn(4, 8)
        store(nc.scalar, FIRST, 7)
        turn(8, 9)
        store(nc.sync, 7, 8)
